import numpy as np
import ml_dtypes


def mxq(x, axis, fmt="e4m3"):
    dtype, down = {"e4m3": (ml_dtypes.float8_e4m3fn, 7), "e5m2": (ml_dtypes.float8_e5m2, 14)}[fmt]
    v = np.moveaxis(np.asarray(x, np.float32).astype(ml_dtypes.bfloat16).astype(np.float64), axis, -1)
    blocks = v.reshape(v.shape[:-1] + (-1, 32))
    amax = np.abs(blocks).max(-1, keepdims=True)
    byte = np.maximum(np.where(amax > 0, np.frexp(amax)[1] - 1 + 127, 0) - down, 1)
    scale = np.exp2(byte - 127.0)
    codes = (blocks / scale).astype(np.float32).astype(dtype).astype(np.float64)
    return np.moveaxis((codes * scale).reshape(v.shape), -1, axis)


WIDE = False


def mx_kscale(k):
    if not WIDE:
        return np.ones(k)
    levels = np.array([10, -10, 5, -5, 0])
    if k % 512:
        return np.exp2(np.random.permutation(np.resize(levels, k // 32))).repeat(32)
    a = np.empty((k // 512, 16))
    for p in range(k // 512):
        a[p, :8] = np.random.permutation(np.resize(levels, 8))
        for g in range(8):
            far = levels[np.abs(levels - a[p, g]) >= 10]
            a[p, g + 8] = far[np.random.randint(len(far))]
    return np.exp2(a.ravel()).repeat(32)


def f64(x):
    return np.asarray(x).astype(np.float64)


def striped8(idx):
    return np.asarray(idx).reshape(8, -1, 16).transpose(0, 2, 1).reshape(128, -1).astype(np.uint16)


def unstriped8(offs):
    return offs.reshape(8, 16, -1).transpose(0, 2, 1).reshape(8, -1).astype(np.int64)


def pick8(x, idx, run):
    r = np.arange(len(x))
    return x[r[:, None], idx[r % (8 * run) // run]]


E2M1 = np.array([0.0, 0.5, 1.0, 1.5, 2.0, 3.0, 4.0, 6.0, -0.0, -0.5, -1.0, -1.5, -2.0, -3.0, -4.0, -6.0])


def pack_weight(w, fmt):
    k, n = w.shape
    w = f64(np.asarray(w, np.float32).astype(ml_dtypes.bfloat16)).reshape(k // 32, 32, n)
    amax = np.abs(w).max(1)
    if fmt == "e4m3":
        byte = np.frexp(amax)[1] - 1 + 127 - 7
    else:
        mant, ex = np.frexp(amax / 6.0)
        byte = np.where(mant > 0.5, ex, ex - 1) + 127
    byte = np.clip(np.where(amax > 0, byte, 1), 1, 254)
    scaled = (w * np.exp2(127.0 - byte)[:, None, :]).reshape(k, n).astype(np.float32)
    by_word = np.ascontiguousarray(scaled.reshape(k // 512, 128, 4, n).transpose(0, 1, 3, 2))
    if fmt == "e4m3":
        words = by_word.astype(ml_dtypes.float8_e4m3fn).view(np.uint8)
    else:
        c = by_word.astype(ml_dtypes.float4_e2m1fn).view(np.uint8) & 0xF
        words = (c[..., 0::2] | (c[..., 1::2] << 4)).reshape(k // 512, 128, 2 * n)
    return np.ascontiguousarray(words), np.ascontiguousarray(byte.astype(np.uint8).reshape(k // 512, 16, n))


def unpack_weight(words, scales, fmt):
    g, _, n = scales.shape
    words = np.ascontiguousarray(words).reshape(g, 128, n, -1)
    if fmt == "e4m3":
        vals = words.view(ml_dtypes.float8_e4m3fn).astype(np.float64)
    else:
        nib = np.empty((g, 128, n, 4), np.uint8)
        nib[..., 0::2] = words & 0xF
        nib[..., 1::2] = words >> 4
        vals = E2M1[nib]
    vals = vals * np.repeat(np.exp2(scales.astype(np.float64) - 127.0), 8, axis=1)[..., None]
    return vals.transpose(0, 1, 3, 2).reshape(g * 512, n)


D, T, Q, I, E = 512, 1024, 128, 512, 512


def setup_inputs():
    n = np.random.standard_normal
    idx = np.stack([np.random.permutation(T)[:I] for _ in range(8)])
    idx2 = np.stack([np.random.permutation(T)[:I] for _ in range(8)])
    fd = mx_kscale(D)
    ft = mx_kscale(T)
    keysp = pack_weight(n((D, T)) / fd[:, None], "e2m1")
    return {
        "query": (n((D, Q)) * 0.4 / np.sqrt(D) * fd[:, None]).astype(np.float32),
        "keys_words": keysp[0],
        "keys_scales": keysp[1],
        "lam": (np.random.uniform(0.3, 1.2, (Q, 1))).astype(np.float32),
        "share": (np.random.uniform(0.3, 1.0, (Q, 1))).astype(np.float32),
        "fac": (np.random.uniform(4.0, 16.0, (1, T)) * ft).astype(np.float32),
        "vals": (n((T, E)) / ft[:, None]).astype(np.float32),
        "offs": striped8(idx),
        "offs2": striped8(idx2),
    }


def reference(query, keys_words, keys_scales, lam, share, fac, vals, offs, offs2):
    idx = unstriped8(offs)
    idx2 = unstriped8(offs2)
    keysu = unpack_weight(keys_words, keys_scales, "e2m1")
    queryq = mxq(f64(query), 0, "e4m3")
    a = queryq.T @ keysu
    s = pick8(a, idx, 16) + pick8(a, idx2, 16) * f64(lam)
    p = np.exp(s - np.max(s, axis=1, keepdims=True))
    w = p / np.sum(p, axis=1, keepdims=True)
    wa = np.zeros((Q, T))
    wa[np.arange(Q)[:, None], idx[np.arange(Q) % 128 // 16]] = w
    wb = np.zeros((Q, T))
    wb[np.arange(Q)[:, None], idx2[np.arange(Q) % 128 // 16]] = w
    wg = (wa + wb * f64(share)) * f64(fac)
    wt = wg.T
    wtq = mxq(wt, 0, "e4m3")
    valsq = mxq(f64(vals), 0, "e4m3")
    o = wtq.T @ valsq
    return o

@@ -1,0 +1,196 @@
+from contextlib import ExitStack
+
+import concourse.mybir as mybir
+from concourse.masks import make_identity
+
+F32 = mybir.dt.float32
+BF16 = mybir.dt.bfloat16
+I32 = mybir.dt.int32
+U32 = mybir.dt.uint32
+U16 = mybir.dt.uint16
+U8 = mybir.dt.uint8
+FP8X4 = mybir.dt.float8_e4m3fn_x4
+FP4X4 = mybir.dt.float4_e2m1fn_x4
+ALU = mybir.AluOpType
+ACT = mybir.ActivationFunctionType
+
+D, T, Q, SLOTS, E = 512, 1024, 128, 512, 512
+FLOPS = 2 * D * Q * T + 2 * T * Q * E
+
+P = 128
+PACK = 4
+K_PASS = P * PACK
+PASSES = T // K_PASS
+SCORE_N = 256
+HALF = SLOTS // 2
+OUT_N = 256
+
+
+def tile_attend_pairreads_heads_kernel(tc, query, keys_words, keys_scales, lam, share, fac, vals, offs, offs2, out):
+    nc = tc.nc
+    with ExitStack() as ctx:
+        keep = ctx.enter_context(tc.tile_pool(name="keep", bufs=1))
+        psum = ctx.enter_context(tc.psum_pool(name="psum", bufs=1))
+
+        list_a = keep.tile([P, SLOTS // 16], U16)
+        list_b = keep.tile([P, SLOTS // 16], U16)
+        q_raw = keep.tile([P, PACK, Q], F32)
+        k_words = keep.tile([P, 2 * T], U8, align_bytes=64)
+        k_scales = keep.tile([P, T], U8, align_bytes=64)
+        lam_col = keep.tile([P, 1], F32)
+        share_col = keep.tile([P, 1], F32, tag="mx_in1", align_bytes=64)
+        fac_cols = keep.tile([P, PASSES, PACK], F32)
+
+        nc.vector.memset(k_scales[:].bitcast(I32), 0)
+        nc.sync.dma_start(out=q_raw[:], in_=query.rearrange("(p j) q -> p j q", j=PACK))
+        nc.sync.dma_start(out=k_words[:].bitcast(I32), in_=keys_words[0].bitcast(I32))
+        for quad in range(4):
+            nc.sync.dma_start(
+                out=k_scales[32 * quad : 32 * quad + 4, :].bitcast(I32),
+                in_=keys_scales[0, 4 * quad : 4 * quad + 4, :].bitcast(I32),
+            )
+        nc.sync.dma_start(list_b[:], offs2)
+        nc.sync.dma_start(list_a[:], offs)
+        nc.sync.dma_start(out=lam_col[:], in_=lam)
+        v_raw = []
+        for g in range(PASSES):
+            raw = keep.tile([P, PACK, E], F32, tag=f"raw{g}")
+            nc.sync.dma_start(
+                out=raw[:], in_=vals[g * K_PASS : (g + 1) * K_PASS, :].rearrange("(p j) e -> p j e", j=PACK)
+            )
+            v_raw.append(raw)
+        nc.sync.dma_start(out=share_col[:], in_=share)
+        nc.sync.dma_start(out=fac_cols[:], in_=fac[0].rearrange("(g p j) -> p g j", g=PASSES, j=PACK))
+
+        warm = keep.tile([P, 2], F32)
+        nc.vector.memset(warm[:], 0.0)
+        warm_out = keep.tile([P, 2], F32)
+        nc.scalar.activation(out=warm_out[:], in_=warm[:], func=ACT.Exp)
+
+        placed_a = keep.tile([P, T], F32)
+        nc.vector.memset(placed_a[:], 0.0)
+        ident = keep.tile([P, P], F32)
+        make_identity(nc, ident[:])
+
+        q_bf = keep.tile([P, Q, PACK], BF16, tag="placed_b", align_bytes=64)
+        nc.vector.tensor_copy(
+            out=q_bf[:].rearrange("p (c i) j -> p c j i", i=4),
+            in_=q_raw[:].rearrange("p j (c i) -> p c j i", i=4),
+        )
+        q_codes = keep.tile([P, Q], U32, align_bytes=64)
+        q_scales = keep.tile([P, Q], U8, align_bytes=64)
+        nc.vector.quantize_mx(out=q_codes[:].bitcast(FP8X4), scales=q_scales[:], in_=q_bf[:].rearrange("p q j -> p (q j)"))
+
+        placed_b = keep.tile([P, T], F32, tag="placed_b", align_bytes=64)
+        nc.vector.memset(placed_b[:], 0.0)
+        scores = keep.tile([P, T], F32)
+        for c in range(T // SCORE_N):
+            cols = slice(c * SCORE_N, (c + 1) * SCORE_N)
+            bank = psum.tile([P, SCORE_N], F32, name=f"score_bank{c}")
+            nc.tensor.matmul_mx(
+                out=bank[:],
+                lhsT=q_codes[:].bitcast(FP8X4),
+                lhsT_scale=q_scales[:],
+                rhs=k_words[:, 2 * cols.start : 2 * cols.stop].bitcast(FP4X4),
+                rhs_scale=k_scales[:, cols],
+                start=True,
+                stop=True,
+            )
+            if c % 2 == 0:
+                nc.scalar.copy(out=scores[:, cols], in_=bank[:])
+            else:
+                nc.vector.tensor_copy(out=scores[:, cols], in_=bank[:])
+
+        second = keep.tile([P, SLOTS], F32, tag="mx_in0", align_bytes=64)
+        second_lam = keep.tile([P, SLOTS], F32)
+        pair = keep.tile([P, SLOTS], F32)
+        halves = [(slice(h * HALF, (h + 1) * HALF), slice(h * HALF // 16, (h + 1) * HALF // 16)) for h in range(2)]
+        for slots, entries in halves:
+            nc.vector.tensor_copy(second[:, slots], scores[:].indirect(list_b[:, entries]))
+            nc.scalar.activation(out=second_lam[:, slots], in_=second[:, slots], func=ACT.Copy, scale=lam_col[:])
+        for slots, entries in halves:
+            nc.vector.tensor_tensor(pair[:, slots], scores[:].indirect(list_a[:, entries]), second_lam[:, slots], ALU.add)
+
+        neg_max = keep.tile([P, 1], F32)
+        nc.vector.tensor_reduce(out=neg_max[:], in_=pair[:], axis=mybir.AxisListType.X, op=ALU.max, negate=True)
+        prob = keep.tile([P, SLOTS], F32)
+        row_sum = keep.tile([P, 1], F32)
+        nc.scalar.activation(out=prob[:], in_=pair[:], func=ACT.Exp, bias=neg_max[:], accum_out=row_sum[:])
+        inv_sum = keep.tile([P, 1], F32)
+        nc.vector.reciprocal(out=inv_sum[:], in_=row_sum[:])
+        nc.vector.tensor_copy(placed_a[:].indirect(list_a[:]), prob[:])
+
+        shared_w = keep.tile([P, SLOTS], F32, tag="v_codes", align_bytes=64)
+        nc.scalar.activation(out=shared_w[:], in_=prob[:], func=ACT.Copy, scale=share_col[:])
+        nc.vector.tensor_copy(placed_b[:].indirect(list_b[:]), shared_w[:])
+
+        v_bf = [keep.tile([P, E, PACK], BF16, tag=f"mx_in{g}", name=f"v_bf{g}", align_bytes=64) for g in range(PASSES)]
+        for g in range(PASSES):
+            for h in range(2):
+                cols = slice(h * E // 2, (h + 1) * E // 2)
+                nc.scalar.copy(
+                    out=v_bf[g][:, cols, :].rearrange("p (c i) j -> p c j i", i=4),
+                    in_=v_raw[g][:, :, cols].rearrange("p j (c i) -> p c j i", i=4),
+                )
+        v_codes = keep.tile([P, PASSES * E], U32, tag="v_codes", align_bytes=64)
+        v_scales = keep.tile([P, PASSES * E], U8, align_bytes=64)
+        for g in range(PASSES):
+            nc.vector.quantize_mx(
+                out=v_codes[:, g * E : (g + 1) * E].bitcast(FP8X4),
+                scales=v_scales[:, g * E : (g + 1) * E],
+                in_=v_bf[g][:].rearrange("p e j -> p (e j)"),
+            )
+
+        inv_rows = psum.tile([P, Q], F32, name="score_bank0")
+        nc.tensor.transpose(inv_rows[:], inv_sum[:].to_broadcast([P, P]), ident[:])
+        factor = keep.tile([P, PASSES, PACK, Q], F32, tag="raw1")
+        for g in range(PASSES):
+            for j in range(PACK):
+                nc.scalar.activation(out=factor[:, g, j, :], in_=inv_rows[:], func=ACT.Copy, scale=fac_cols[:, g, j : j + 1])
+
+        turned = [psum.tile([P, PACK, Q], F32, name=f"turned{g}") for g in range(PASSES)]
+        for placed in (placed_a, placed_b):
+            for g in range(PASSES):
+                for j in range(PACK):
+                    nc.tensor.matmul(
+                        turned[g][:, j, :],
+                        lhsT=placed[:, g * K_PASS + j : (g + 1) * K_PASS : PACK],
+                        rhs=ident[:],
+                        start=(placed is placed_a and j == 0),
+                        stop=(placed is placed_b and j == PACK - 1),
+                        is_transpose=True,
+                    )
+
+        w_bf = keep.tile([P, PASSES, Q, PACK], BF16, tag="mx_in1", align_bytes=64)
+        for g in range(PASSES):
+            nc.vector.tensor_tensor(
+                w_bf[:, g, :, :],
+                turned[g][:].rearrange("p j q -> p q j"),
+                factor[:, g, :, :].rearrange("p j q -> p q j"),
+                ALU.mult,
+            )
+        w_codes = keep.tile([P, PASSES, Q], U32, align_bytes=64)
+        w_scales = keep.tile([P, PASSES, Q], U8, align_bytes=64)
+        for g in range(PASSES):
+            nc.vector.quantize_mx(
+                out=w_codes[:, g, :].bitcast(FP8X4), scales=w_scales[:, g, :], in_=w_bf[:, g, :, :].rearrange("p q j -> p (q j)")
+            )
+
+        out_banks = [psum.tile([P, OUT_N], F32, name=f"out_bank{h}") for h in range(E // OUT_N)]
+        for g in range(PASSES):
+            for h in range(E // OUT_N):
+                cols = slice(g * E + h * OUT_N, g * E + (h + 1) * OUT_N)
+                nc.tensor.matmul_mx(
+                    out=out_banks[h][:],
+                    lhsT=w_codes[:, g, :].bitcast(FP8X4),
+                    lhsT_scale=w_scales[:, g, :],
+                    rhs=v_codes[:, cols].bitcast(FP8X4),
+                    rhs_scale=v_scales[:, cols],
+                    start=(g == 0),
+                    stop=(g == PASSES - 1),
+                )
+        result = [keep.tile([P, OUT_N], F32, name=f"result{h}") for h in range(E // OUT_N)]
+        nc.vector.tensor_copy(out=result[0][:], in_=out_banks[0][:])
+        nc.sync.dma_start(out=out[:, 0:OUT_N], in_=result[0][:])
+        nc.scalar.copy(out=result[1][:], in_=out_banks[1][:])
+        nc.scalar.dma_start(out=out[:, OUT_N:E], in_=result[1][:])

@@ -52,13 +52,13 @@ def tile_attend_pairreads_heads_kernel(tc, query, keys_words, keys_scales, lam, 
         nc.sync.dma_start(list_b[:], offs2)
         nc.sync.dma_start(list_a[:], offs)
         nc.sync.dma_start(out=lam_col[:], in_=lam)
-        v_raw = []
+        v_raw = {}
         for g in range(PASSES):
-            raw = keep.tile([P, PACK, E], F32, tag=f"raw{g}")
-            nc.sync.dma_start(
-                out=raw[:], in_=vals[g * K_PASS : (g + 1) * K_PASS, :].rearrange("(p j) e -> p j e", j=PACK)
-            )
-            v_raw.append(raw)
+            rows = vals[g * K_PASS : (g + 1) * K_PASS, :].rearrange("(p j) e -> p j e", j=PACK)
+            for h in range(2):
+                raw = keep.tile([P, PACK, E // 2], F32, tag=f"raw{g}{h}", align_bytes=64)
+                nc.sync.dma_start(out=raw[:], in_=rows[:, :, h * E // 2 : (h + 1) * E // 2])
+                v_raw[g, h] = raw
         nc.sync.dma_start(out=share_col[:], in_=share)
         nc.sync.dma_start(out=fac_cols[:], in_=fac[0].rearrange("(g p j) -> p g j", g=PASSES, j=PACK))
 
@@ -67,7 +67,7 @@ def tile_attend_pairreads_heads_kernel(tc, query, keys_words, keys_scales, lam, 
         warm_out = keep.tile([P, 2], F32)
         nc.scalar.activation(out=warm_out[:], in_=warm[:], func=ACT.Exp)
 
-        placed_a = keep.tile([P, T], F32)
+        placed_a = keep.tile([P, T], F32, tag="placed_a")
         nc.vector.memset(placed_a[:], 0.0)
         ident = keep.tile([P, P], F32)
         make_identity(nc, ident[:])
@@ -120,7 +120,7 @@ def tile_attend_pairreads_heads_kernel(tc, query, keys_words, keys_scales, lam, 
         nc.vector.reciprocal(out=inv_sum[:], in_=row_sum[:])
         nc.vector.tensor_copy(placed_a[:].indirect(list_a[:]), prob[:])
 
-        shared_w = keep.tile([P, SLOTS], F32, tag="v_codes", align_bytes=64)
+        shared_w = keep.tile([P, SLOTS], F32)
         nc.scalar.activation(out=shared_w[:], in_=prob[:], func=ACT.Copy, scale=share_col[:])
         nc.vector.tensor_copy(placed_b[:].indirect(list_b[:]), shared_w[:])
 
@@ -130,9 +130,9 @@ def tile_attend_pairreads_heads_kernel(tc, query, keys_words, keys_scales, lam, 
                 cols = slice(h * E // 2, (h + 1) * E // 2)
                 nc.scalar.copy(
                     out=v_bf[g][:, cols, :].rearrange("p (c i) j -> p c j i", i=4),
-                    in_=v_raw[g][:, :, cols].rearrange("p j (c i) -> p c j i", i=4),
+                    in_=v_raw[g, h][:].rearrange("p j (c i) -> p c j i", i=4),
                 )
-        v_codes = keep.tile([P, PASSES * E], U32, tag="v_codes", align_bytes=64)
+        v_codes = keep.tile([P, PASSES * E], U32, tag="raw10", align_bytes=64)
         v_scales = keep.tile([P, PASSES * E], U8, align_bytes=64)
         for g in range(PASSES):
             nc.vector.quantize_mx(
@@ -141,40 +141,57 @@ def tile_attend_pairreads_heads_kernel(tc, query, keys_words, keys_scales, lam, 
                 in_=v_bf[g][:].rearrange("p e j -> p (e j)"),
             )
 
-        inv_rows = psum.tile([P, Q], F32, name="score_bank0")
-        nc.tensor.transpose(inv_rows[:], inv_sum[:].to_broadcast([P, P]), ident[:])
-        factor = keep.tile([P, PASSES, PACK, Q], F32, tag="raw1")
+        dealt_a = keep.tile([P, PASSES, PACK, P], F32, tag="raw11", align_bytes=64)
+        nc.scalar.activation(
+            out=dealt_a[:].rearrange("q g j p -> q g p j"),
+            in_=placed_a[:].rearrange("q (g p j) -> q g p j", g=PASSES, j=PACK),
+            func=ACT.Copy,
+            scale=inv_sum[:],
+        )
+        dealt_b = keep.tile([P, PASSES, PACK, P], F32, tag="placed_a")
         for g in range(PASSES):
-            for j in range(PACK):
-                nc.scalar.activation(out=factor[:, g, j, :], in_=inv_rows[:], func=ACT.Copy, scale=fac_cols[:, g, j : j + 1])
+            nc.scalar.activation(
+                out=dealt_b[:, g, :, :].rearrange("q j p -> q p j"),
+                in_=placed_b[:, g * K_PASS : (g + 1) * K_PASS].rearrange("q (p j) -> q p j", j=PACK),
+                func=ACT.Copy,
+                scale=inv_sum[:],
+            )
 
         turned = [psum.tile([P, PACK, Q], F32, name=f"turned{g}") for g in range(PASSES)]
-        for placed in (placed_a, placed_b):
+        for dealt in (dealt_a, dealt_b):
             for g in range(PASSES):
                 for j in range(PACK):
                     nc.tensor.matmul(
                         turned[g][:, j, :],
-                        lhsT=placed[:, g * K_PASS + j : (g + 1) * K_PASS : PACK],
+                        lhsT=dealt[:, g, j, :],
                         rhs=ident[:],
-                        start=(placed is placed_a and j == 0),
-                        stop=(placed is placed_b and j == PACK - 1),
+                        start=(dealt is dealt_a and j == 0),
+                        stop=(dealt is dealt_b and j == PACK - 1),
                         is_transpose=True,
                     )
 
         w_bf = keep.tile([P, PASSES, Q, PACK], BF16, tag="mx_in1", align_bytes=64)
-        for g in range(PASSES):
-            nc.vector.tensor_tensor(
-                w_bf[:, g, :, :],
-                turned[g][:].rearrange("p j q -> p q j"),
-                factor[:, g, :, :].rearrange("p j q -> p q j"),
-                ALU.mult,
-            )
         w_codes = keep.tile([P, PASSES, Q], U32, align_bytes=64)
         w_scales = keep.tile([P, PASSES, Q], U8, align_bytes=64)
-        for g in range(PASSES):
+
+        def weigh(g, rows):
+            nc.vector.tensor_tensor(
+                w_bf[:, g, rows, :],
+                turned[g][:, :, rows].rearrange("p j q -> p q j"),
+                fac_cols[:, g, :].unsqueeze(1).to_broadcast([P, rows.stop - rows.start, PACK]),
+                ALU.mult,
+            )
+
+        def quantize_weights(g):
             nc.vector.quantize_mx(
                 out=w_codes[:, g, :].bitcast(FP8X4), scales=w_scales[:, g, :], in_=w_bf[:, g, :, :].rearrange("p q j -> p (q j)")
             )
+
+        weigh(0, slice(0, Q))
+        weigh(1, slice(0, Q // 2))
+        quantize_weights(0)
+        weigh(1, slice(Q // 2, Q))
+        quantize_weights(1)
 
         out_banks = [psum.tile([P, OUT_N], F32, name=f"out_bank{h}") for h in range(E // OUT_N)]
         for g in range(PASSES):

@@ -24,6 +24,7 @@ PASSES = T // K_PASS
 SCORE_N = 256
 HALF = SLOTS // 2
 OUT_N = 256
+LEAD = 128
 
 
 def tile_attend_pairreads_heads_kernel(tc, query, keys_words, keys_scales, lam, share, fac, vals, offs, offs2, out):
@@ -34,12 +35,9 @@ def tile_attend_pairreads_heads_kernel(tc, query, keys_words, keys_scales, lam, 
 
         list_a = keep.tile([P, SLOTS // 16], U16)
         list_b = keep.tile([P, SLOTS // 16], U16)
-        q_raw = keep.tile([P, PACK, Q], F32)
-        k_words = keep.tile([P, 2 * T], U8, align_bytes=64)
-        k_scales = keep.tile([P, T], U8, align_bytes=64)
-        lam_col = keep.tile([P, 1], F32)
-        share_col = keep.tile([P, 1], F32, tag="mx_in1", align_bytes=64)
-        fac_cols = keep.tile([P, PASSES, PACK], F32)
+        q_raw = keep.tile([P, PACK, Q], F32, tag="raw01", align_bytes=64)
+        k_words = keep.tile([P, 2 * T], U8, tag="raw10", align_bytes=64)
+        k_scales = keep.tile([P, T], U8, tag="raw11", align_bytes=64)
 
         nc.vector.memset(k_scales[:].bitcast(I32), 0)
         nc.sync.dma_start(out=q_raw[:], in_=query.rearrange("(p j) q -> p j q", j=PACK))
@@ -51,35 +49,32 @@ def tile_attend_pairreads_heads_kernel(tc, query, keys_words, keys_scales, lam, 
             )
         nc.sync.dma_start(list_b[:], offs2)
         nc.sync.dma_start(list_a[:], offs)
-        nc.sync.dma_start(out=lam_col[:], in_=lam)
-        v_raw = {}
-        for g in range(PASSES):
-            rows = vals[g * K_PASS : (g + 1) * K_PASS, :].rearrange("(p j) e -> p j e", j=PACK)
-            for h in range(2):
-                raw = keep.tile([P, PACK, E // 2], F32, tag=f"raw{g}{h}", align_bytes=64)
-                nc.sync.dma_start(out=raw[:], in_=rows[:, :, h * E // 2 : (h + 1) * E // 2])
-                v_raw[g, h] = raw
-        nc.sync.dma_start(out=share_col[:], in_=share)
-        nc.sync.dma_start(out=fac_cols[:], in_=fac[0].rearrange("(g p j) -> p g j", g=PASSES, j=PACK))
 
-        warm = keep.tile([P, 2], F32)
+        warm = keep.tile([P, 2], F32, tag="lam")
         nc.vector.memset(warm[:], 0.0)
-        warm_out = keep.tile([P, 2], F32)
+        warm_out = keep.tile([P, 2], F32, tag="raw00", align_bytes=64)
         nc.scalar.activation(out=warm_out[:], in_=warm[:], func=ACT.Exp)
 
-        placed_a = keep.tile([P, T], F32, tag="placed_a")
+        placed_lead = keep.tile([P, T], F32)
+        nc.vector.memset(placed_lead[:], 0.0)
+        placed_a = keep.tile([P, T], F32)
         nc.vector.memset(placed_a[:], 0.0)
         ident = keep.tile([P, P], F32)
         make_identity(nc, ident[:])
 
         q_bf = keep.tile([P, Q, PACK], BF16, tag="placed_b", align_bytes=64)
-        nc.vector.tensor_copy(
-            out=q_bf[:].rearrange("p (c i) j -> p c j i", i=4),
-            in_=q_raw[:].rearrange("p j (c i) -> p c j i", i=4),
-        )
-        q_codes = keep.tile([P, Q], U32, align_bytes=64)
-        q_scales = keep.tile([P, Q], U8, align_bytes=64)
-        nc.vector.quantize_mx(out=q_codes[:].bitcast(FP8X4), scales=q_scales[:], in_=q_bf[:].rearrange("p q j -> p (q j)"))
+        q_codes = keep.tile([P, Q], U32, tag="dealt", align_bytes=64)
+        q_scales = keep.tile([P, Q], U8, tag="mx_in1", align_bytes=64)
+        q_halves = [slice(0, Q // 2), slice(Q // 2, Q)]
+        for rows in q_halves:
+            nc.vector.tensor_copy(
+                out=q_bf[:, rows, :].rearrange("p (c i) j -> p c j i", i=4),
+                in_=q_raw[:, :, rows].rearrange("p j (c i) -> p c j i", i=4),
+            )
+        for rows in q_halves:
+            nc.vector.quantize_mx(
+                out=q_codes[:, rows].bitcast(FP8X4), scales=q_scales[:, rows], in_=q_bf[:, rows, :].rearrange("p q j -> p (q j)")
+            )
 
         placed_b = keep.tile([P, T], F32, tag="placed_b", align_bytes=64)
         nc.vector.memset(placed_b[:], 0.0)
@@ -101,6 +96,20 @@ def tile_attend_pairreads_heads_kernel(tc, query, keys_words, keys_scales, lam, 
             else:
                 nc.vector.tensor_copy(out=scores[:, cols], in_=bank[:])
 
+        lam_col = keep.tile([P, 1], F32, tag="lam")
+        nc.sync.dma_start(out=lam_col[:], in_=lam)
+        v_raw = {}
+        for g in range(PASSES):
+            rows = vals[g * K_PASS : (g + 1) * K_PASS, :].rearrange("(p j) e -> p j e", j=PACK)
+            for h in range(2):
+                raw = keep.tile([P, PACK, E // 2], F32, tag=f"raw{g}{h}", align_bytes=64)
+                nc.sync.dma_start(out=raw[:], in_=rows[:, :, h * E // 2 : (h + 1) * E // 2])
+                v_raw[g, h] = raw
+        share_col = keep.tile([P, 1], F32, tag="mx_in1", align_bytes=64)
+        nc.sync.dma_start(out=share_col[:], in_=share)
+        fac_cols = keep.tile([P, PASSES, PACK], F32, tag="dealt", align_bytes=64)
+        nc.sync.dma_start(out=fac_cols[:], in_=fac[0].rearrange("(g p j) -> p g j", g=PASSES, j=PACK))
+
         second = keep.tile([P, SLOTS], F32, tag="mx_in0", align_bytes=64)
         second_lam = keep.tile([P, SLOTS], F32)
         pair = keep.tile([P, SLOTS], F32)
@@ -114,11 +123,14 @@ def tile_attend_pairreads_heads_kernel(tc, query, keys_words, keys_scales, lam, 
         neg_max = keep.tile([P, 1], F32)
         nc.vector.tensor_reduce(out=neg_max[:], in_=pair[:], axis=mybir.AxisListType.X, op=ALU.max, negate=True)
         prob = keep.tile([P, SLOTS], F32)
+        prob_lead = keep.tile([P, LEAD], F32)
+        nc.scalar.activation(out=prob_lead[:], in_=pair[:, :LEAD], func=ACT.Exp, bias=neg_max[:])
+        nc.vector.tensor_copy(placed_lead[:].indirect(list_a[:, : LEAD // 16]), prob_lead[:])
         row_sum = keep.tile([P, 1], F32)
         nc.scalar.activation(out=prob[:], in_=pair[:], func=ACT.Exp, bias=neg_max[:], accum_out=row_sum[:])
         inv_sum = keep.tile([P, 1], F32)
         nc.vector.reciprocal(out=inv_sum[:], in_=row_sum[:])
-        nc.vector.tensor_copy(placed_a[:].indirect(list_a[:]), prob[:])
+        nc.vector.tensor_copy(placed_a[:].indirect(list_a[:, LEAD // 16 :]), prob[:, LEAD:])
 
         shared_w = keep.tile([P, SLOTS], F32)
         nc.scalar.activation(out=shared_w[:], in_=prob[:], func=ACT.Copy, scale=share_col[:])
@@ -132,53 +144,58 @@ def tile_attend_pairreads_heads_kernel(tc, query, keys_words, keys_scales, lam, 
                     out=v_bf[g][:, cols, :].rearrange("p (c i) j -> p c j i", i=4),
                     in_=v_raw[g, h][:].rearrange("p j (c i) -> p c j i", i=4),
                 )
-        v_codes = keep.tile([P, PASSES * E], U32, tag="raw10", align_bytes=64)
-        v_scales = keep.tile([P, PASSES * E], U8, align_bytes=64)
-        for g in range(PASSES):
+        first_codes = keep.tile([P, OUT_N], U32, align_bytes=64)
+        rest_codes = keep.tile([P, 3, OUT_N], U32, tag="raw10", align_bytes=64)
+        v_scales = keep.tile([P, PASSES, E], U8, align_bytes=64)
+        v_codes = {(0, 0): first_codes[:], (0, 1): rest_codes[:, 0, :], (1, 0): rest_codes[:, 1, :], (1, 1): rest_codes[:, 2, :]}
+        for h in range(2):
+            cols = slice(h * OUT_N, (h + 1) * OUT_N)
             nc.vector.quantize_mx(
-                out=v_codes[:, g * E : (g + 1) * E].bitcast(FP8X4),
-                scales=v_scales[:, g * E : (g + 1) * E],
-                in_=v_bf[g][:].rearrange("p e j -> p (e j)"),
+                out=v_codes[0, h].bitcast(FP8X4), scales=v_scales[:, 0, cols], in_=v_bf[0][:, cols, :].rearrange("p e j -> p (e j)")
             )
-
-        dealt_a = keep.tile([P, PASSES, PACK, P], F32, tag="raw11", align_bytes=64)
-        nc.scalar.activation(
-            out=dealt_a[:].rearrange("q g j p -> q g p j"),
-            in_=placed_a[:].rearrange("q (g p j) -> q g p j", g=PASSES, j=PACK),
-            func=ACT.Copy,
-            scale=inv_sum[:],
+        nc.vector.quantize_mx(
+            out=rest_codes[:, 1:, :].rearrange("p h e -> p (h e)").bitcast(FP8X4),
+            scales=v_scales[:, 1, :],
+            in_=v_bf[1][:].rearrange("p e j -> p (e j)"),
         )
-        dealt_b = keep.tile([P, PASSES, PACK, P], F32, tag="placed_a")
+
+        inv_rows = psum.tile([P, Q], F32, name="score_bank0")
+        nc.tensor.transpose(inv_rows[:], inv_sum[:].to_broadcast([P, P]), ident[:])
+        factor = keep.tile([P, PASSES, PACK, Q], F32, tag="raw11", align_bytes=64)
         for g in range(PASSES):
-            nc.scalar.activation(
-                out=dealt_b[:, g, :, :].rearrange("q j p -> q p j"),
-                in_=placed_b[:, g * K_PASS : (g + 1) * K_PASS].rearrange("q (p j) -> q p j", j=PACK),
-                func=ACT.Copy,
-                scale=inv_sum[:],
-            )
+            for j in range(PACK):
+                nc.scalar.activation(out=factor[:, g, j, :], in_=inv_rows[:], func=ACT.Copy, scale=fac_cols[:, g, j : j + 1])
+        dealt = keep.tile([P, PACK, P], F32, tag="dealt", align_bytes=64)
+        nc.scalar.copy(
+            out=dealt[:].rearrange("q j p -> q p j"), in_=placed_b[:, K_PASS:].rearrange("q (p j) -> q p j", j=PACK)
+        )
 
         turned = [psum.tile([P, PACK, Q], F32, name=f"turned{g}") for g in range(PASSES)]
-        for dealt in (dealt_a, dealt_b):
+        for placed in (placed_lead, placed_a, placed_b):
             for g in range(PASSES):
                 for j in range(PACK):
+                    if placed is placed_b and g == 1:
+                        columns = dealt[:, j, :]
+                    else:
+                        columns = placed[:, g * K_PASS + j : (g + 1) * K_PASS : PACK]
                     nc.tensor.matmul(
                         turned[g][:, j, :],
-                        lhsT=dealt[:, g, j, :],
+                        lhsT=columns,
                         rhs=ident[:],
-                        start=(dealt is dealt_a and j == 0),
-                        stop=(dealt is dealt_b and j == PACK - 1),
+                        start=(placed is placed_lead and j == 0),
+                        stop=(placed is placed_b and j == PACK - 1),
                         is_transpose=True,
                     )
 
         w_bf = keep.tile([P, PASSES, Q, PACK], BF16, tag="mx_in1", align_bytes=64)
-        w_codes = keep.tile([P, PASSES, Q], U32, align_bytes=64)
+        w_codes = keep.tile([P, PASSES, Q], U32, tag="dealt", align_bytes=64)
         w_scales = keep.tile([P, PASSES, Q], U8, align_bytes=64)
 
         def weigh(g, rows):
             nc.vector.tensor_tensor(
                 w_bf[:, g, rows, :],
                 turned[g][:, :, rows].rearrange("p j q -> p q j"),
-                fac_cols[:, g, :].unsqueeze(1).to_broadcast([P, rows.stop - rows.start, PACK]),
+                factor[:, g, :, rows].rearrange("p j q -> p q j"),
                 ALU.mult,
             )
 
@@ -196,13 +213,13 @@ def tile_attend_pairreads_heads_kernel(tc, query, keys_words, keys_scales, lam, 
         out_banks = [psum.tile([P, OUT_N], F32, name=f"out_bank{h}") for h in range(E // OUT_N)]
         for g in range(PASSES):
             for h in range(E // OUT_N):
-                cols = slice(g * E + h * OUT_N, g * E + (h + 1) * OUT_N)
+                cols = slice(h * OUT_N, (h + 1) * OUT_N)
                 nc.tensor.matmul_mx(
                     out=out_banks[h][:],
                     lhsT=w_codes[:, g, :].bitcast(FP8X4),
                     lhsT_scale=w_scales[:, g, :],
-                    rhs=v_codes[:, cols].bitcast(FP8X4),
-                    rhs_scale=v_scales[:, cols],
+                    rhs=v_codes[g, h].bitcast(FP8X4),
+                    rhs_scale=v_scales[:, g, cols],
                     start=(g == 0),
                     stop=(g == PASSES - 1),
                 )

@@ -91,10 +91,7 @@ def tile_attend_pairreads_heads_kernel(tc, query, keys_words, keys_scales, lam, 
                 start=True,
                 stop=True,
             )
-            if c % 2 == 0:
-                nc.scalar.copy(out=scores[:, cols], in_=bank[:])
-            else:
-                nc.vector.tensor_copy(out=scores[:, cols], in_=bank[:])
+            nc.vector.tensor_copy(out=scores[:, cols], in_=bank[:])
 
         lam_col = keep.tile([P, 1], F32, tag="lam")
         nc.sync.dma_start(out=lam_col[:], in_=lam)
@@ -111,7 +108,7 @@ def tile_attend_pairreads_heads_kernel(tc, query, keys_words, keys_scales, lam, 
         nc.sync.dma_start(out=fac_cols[:], in_=fac[0].rearrange("(g p j) -> p g j", g=PASSES, j=PACK))
 
         second = keep.tile([P, SLOTS], F32, tag="mx_in0", align_bytes=64)
-        second_lam = keep.tile([P, SLOTS], F32)
+        second_lam = keep.tile([P, SLOTS], F32, tag="first_codes", align_bytes=64)
         pair = keep.tile([P, SLOTS], F32)
         halves = [(slice(h * HALF, (h + 1) * HALF), slice(h * HALF // 16, (h + 1) * HALF // 16)) for h in range(2)]
         for slots, entries in halves:
@@ -136,27 +133,29 @@ def tile_attend_pairreads_heads_kernel(tc, query, keys_words, keys_scales, lam, 
         nc.scalar.activation(out=shared_w[:], in_=prob[:], func=ACT.Copy, scale=share_col[:])
         nc.vector.tensor_copy(placed_b[:].indirect(list_b[:]), shared_w[:])
 
-        v_bf = [keep.tile([P, E, PACK], BF16, tag=f"mx_in{g}", name=f"v_bf{g}", align_bytes=64) for g in range(PASSES)]
+        first_bf = keep.tile([P, OUT_N, PACK], BF16, align_bytes=64)
+        next_bf = keep.tile([P, OUT_N, PACK], BF16, tag="mx_in0", align_bytes=64)
+        last_bf = keep.tile([P, E, PACK], BF16, tag="mx_in1", align_bytes=64)
+        v_bf = {(0, 0): first_bf[:], (0, 1): next_bf[:], (1, 0): last_bf[:, :OUT_N, :], (1, 1): last_bf[:, OUT_N:, :]}
         for g in range(PASSES):
             for h in range(2):
-                cols = slice(h * E // 2, (h + 1) * E // 2)
                 nc.scalar.copy(
-                    out=v_bf[g][:, cols, :].rearrange("p (c i) j -> p c j i", i=4),
+                    out=v_bf[g, h].rearrange("p (c i) j -> p c j i", i=4),
                     in_=v_raw[g, h][:].rearrange("p j (c i) -> p c j i", i=4),
                 )
-        first_codes = keep.tile([P, OUT_N], U32, align_bytes=64)
+        first_codes = keep.tile([P, OUT_N], U32, tag="first_codes", align_bytes=64)
         rest_codes = keep.tile([P, 3, OUT_N], U32, tag="raw10", align_bytes=64)
         v_scales = keep.tile([P, PASSES, E], U8, align_bytes=64)
         v_codes = {(0, 0): first_codes[:], (0, 1): rest_codes[:, 0, :], (1, 0): rest_codes[:, 1, :], (1, 1): rest_codes[:, 2, :]}
         for h in range(2):
             cols = slice(h * OUT_N, (h + 1) * OUT_N)
             nc.vector.quantize_mx(
-                out=v_codes[0, h].bitcast(FP8X4), scales=v_scales[:, 0, cols], in_=v_bf[0][:, cols, :].rearrange("p e j -> p (e j)")
+                out=v_codes[0, h].bitcast(FP8X4), scales=v_scales[:, 0, cols], in_=v_bf[0, h].rearrange("p e j -> p (e j)")
             )
         nc.vector.quantize_mx(
             out=rest_codes[:, 1:, :].rearrange("p h e -> p (h e)").bitcast(FP8X4),
             scales=v_scales[:, 1, :],
-            in_=v_bf[1][:].rearrange("p e j -> p (e j)"),
+            in_=last_bf[:].rearrange("p e j -> p (e j)"),
         )
 
         inv_rows = psum.tile([P, Q], F32, name="score_bank0")

from contextlib import ExitStack

import concourse.mybir as mybir
from concourse.masks import make_identity

F32 = mybir.dt.float32
BF16 = mybir.dt.bfloat16
I32 = mybir.dt.int32
U32 = mybir.dt.uint32
U16 = mybir.dt.uint16
U8 = mybir.dt.uint8
FP8X4 = mybir.dt.float8_e4m3fn_x4
FP4X4 = mybir.dt.float4_e2m1fn_x4
ALU = mybir.AluOpType
ACT = mybir.ActivationFunctionType

D, T, Q, SLOTS, E = 512, 1024, 128, 512, 512
FLOPS = 2 * D * Q * T + 2 * T * Q * E

P = 128
PACK = 4
K_PASS = P * PACK
PASSES = T // K_PASS
SCORE_N = 256
HALF = SLOTS // 2
OUT_N = 256
LEAD = 128


def tile_attend_pairreads_heads_kernel(tc, query, keys_words, keys_scales, lam, share, fac, vals, offs, offs2, out):
    nc = tc.nc
    with ExitStack() as ctx:
        keep = ctx.enter_context(tc.tile_pool(name="keep", bufs=1))
        psum = ctx.enter_context(tc.psum_pool(name="psum", bufs=1))

        list_a = keep.tile([P, SLOTS // 16], U16)
        list_b = keep.tile([P, SLOTS // 16], U16)
        q_raw = keep.tile([P, PACK, Q], F32, tag="raw01", align_bytes=64)
        k_words = keep.tile([P, 2 * T], U8, tag="raw10", align_bytes=64)
        k_scales = keep.tile([P, T], U8, tag="raw11", align_bytes=64)

        nc.vector.memset(k_scales[:].bitcast(I32), 0)
        nc.sync.dma_start(out=q_raw[:], in_=query.rearrange("(p j) q -> p j q", j=PACK))
        nc.sync.dma_start(out=k_words[:].bitcast(I32), in_=keys_words[0].bitcast(I32))
        for quad in range(4):
            nc.sync.dma_start(
                out=k_scales[32 * quad : 32 * quad + 4, :].bitcast(I32),
                in_=keys_scales[0, 4 * quad : 4 * quad + 4, :].bitcast(I32),
            )
        nc.sync.dma_start(list_b[:], offs2)
        nc.sync.dma_start(list_a[:], offs)

        warm = keep.tile([P, 2], F32, tag="lam")
        nc.vector.memset(warm[:], 0.0)
        warm_out = keep.tile([P, 2], F32, tag="raw00", align_bytes=64)
        nc.scalar.activation(out=warm_out[:], in_=warm[:], func=ACT.Exp)

        placed_lead = keep.tile([P, T], F32)
        nc.vector.memset(placed_lead[:], 0.0)
        placed_a = keep.tile([P, T], F32)
        nc.vector.memset(placed_a[:], 0.0)
        ident = keep.tile([P, P], F32)
        make_identity(nc, ident[:])

        q_bf = keep.tile([P, Q, PACK], BF16, tag="placed_b", align_bytes=64)
        q_codes = keep.tile([P, Q], U32, tag="dealt", align_bytes=64)
        q_scales = keep.tile([P, Q], U8, tag="mx_in1", align_bytes=64)
        q_halves = [slice(0, Q // 2), slice(Q // 2, Q)]
        for rows in q_halves:
            nc.vector.tensor_copy(
                out=q_bf[:, rows, :].rearrange("p (c i) j -> p c j i", i=4),
                in_=q_raw[:, :, rows].rearrange("p j (c i) -> p c j i", i=4),
            )
        for rows in q_halves:
            nc.vector.quantize_mx(
                out=q_codes[:, rows].bitcast(FP8X4), scales=q_scales[:, rows], in_=q_bf[:, rows, :].rearrange("p q j -> p (q j)")
            )

        placed_b = keep.tile([P, T], F32, tag="placed_b", align_bytes=64)
        nc.vector.memset(placed_b[:], 0.0)
        scores = keep.tile([P, T], F32)
        for c in range(T // SCORE_N):
            cols = slice(c * SCORE_N, (c + 1) * SCORE_N)
            bank = psum.tile([P, SCORE_N], F32, name=f"score_bank{c}")
            nc.tensor.matmul_mx(
                out=bank[:],
                lhsT=q_codes[:].bitcast(FP8X4),
                lhsT_scale=q_scales[:],
                rhs=k_words[:, 2 * cols.start : 2 * cols.stop].bitcast(FP4X4),
                rhs_scale=k_scales[:, cols],
                start=True,
                stop=True,
            )
            nc.vector.tensor_copy(out=scores[:, cols], in_=bank[:])

        lam_col = keep.tile([P, 1], F32, tag="lam")
        nc.sync.dma_start(out=lam_col[:], in_=lam)
        v_raw = {}
        for g in range(PASSES):
            rows = vals[g * K_PASS : (g + 1) * K_PASS, :].rearrange("(p j) e -> p j e", j=PACK)
            for h in range(2):
                raw = keep.tile([P, PACK, E // 2], F32, tag=f"raw{g}{h}", align_bytes=64)
                nc.sync.dma_start(out=raw[:], in_=rows[:, :, h * E // 2 : (h + 1) * E // 2])
                v_raw[g, h] = raw
        share_col = keep.tile([P, 1], F32, tag="mx_in1", align_bytes=64)
        nc.sync.dma_start(out=share_col[:], in_=share)
        fac_cols = keep.tile([P, PASSES, PACK], F32, tag="dealt", align_bytes=64)
        nc.sync.dma_start(out=fac_cols[:], in_=fac[0].rearrange("(g p j) -> p g j", g=PASSES, j=PACK))

        second = keep.tile([P, SLOTS], F32, tag="mx_in0", align_bytes=64)
        second_lam = keep.tile([P, SLOTS], F32, tag="first_codes", align_bytes=64)
        pair = keep.tile([P, SLOTS], F32)
        halves = [(slice(h * HALF, (h + 1) * HALF), slice(h * HALF // 16, (h + 1) * HALF // 16)) for h in range(2)]
        for slots, entries in halves:
            nc.vector.tensor_copy(second[:, slots], scores[:].indirect(list_b[:, entries]))
            nc.scalar.activation(out=second_lam[:, slots], in_=second[:, slots], func=ACT.Copy, scale=lam_col[:])
        for slots, entries in halves:
            nc.vector.tensor_tensor(pair[:, slots], scores[:].indirect(list_a[:, entries]), second_lam[:, slots], ALU.add)

        neg_max = keep.tile([P, 1], F32)
        nc.vector.tensor_reduce(out=neg_max[:], in_=pair[:], axis=mybir.AxisListType.X, op=ALU.max, negate=True)
        prob = keep.tile([P, SLOTS], F32)
        prob_lead = keep.tile([P, LEAD], F32)
        nc.scalar.activation(out=prob_lead[:], in_=pair[:, :LEAD], func=ACT.Exp, bias=neg_max[:])
        nc.vector.tensor_copy(placed_lead[:].indirect(list_a[:, : LEAD // 16]), prob_lead[:])
        row_sum = keep.tile([P, 1], F32)
        nc.scalar.activation(out=prob[:], in_=pair[:], func=ACT.Exp, bias=neg_max[:], accum_out=row_sum[:])
        inv_sum = keep.tile([P, 1], F32)
        nc.vector.reciprocal(out=inv_sum[:], in_=row_sum[:])
        nc.vector.tensor_copy(placed_a[:].indirect(list_a[:, LEAD // 16 :]), prob[:, LEAD:])

        shared_w = keep.tile([P, SLOTS], F32)
        nc.scalar.activation(out=shared_w[:], in_=prob[:], func=ACT.Copy, scale=share_col[:])
        nc.vector.tensor_copy(placed_b[:].indirect(list_b[:]), shared_w[:])

        first_bf = keep.tile([P, OUT_N, PACK], BF16, align_bytes=64)
        next_bf = keep.tile([P, OUT_N, PACK], BF16, tag="mx_in0", align_bytes=64)
        last_bf = keep.tile([P, E, PACK], BF16, tag="mx_in1", align_bytes=64)
        v_bf = {(0, 0): first_bf[:], (0, 1): next_bf[:], (1, 0): last_bf[:, :OUT_N, :], (1, 1): last_bf[:, OUT_N:, :]}
        for g in range(PASSES):
            for h in range(2):
                nc.scalar.copy(
                    out=v_bf[g, h].rearrange("p (c i) j -> p c j i", i=4),
                    in_=v_raw[g, h][:].rearrange("p j (c i) -> p c j i", i=4),
                )
        first_codes = keep.tile([P, OUT_N], U32, tag="first_codes", align_bytes=64)
        rest_codes = keep.tile([P, 3, OUT_N], U32, tag="raw10", align_bytes=64)
        v_scales = keep.tile([P, PASSES, E], U8, align_bytes=64)
        v_codes = {(0, 0): first_codes[:], (0, 1): rest_codes[:, 0, :], (1, 0): rest_codes[:, 1, :], (1, 1): rest_codes[:, 2, :]}
        for h in range(2):
            cols = slice(h * OUT_N, (h + 1) * OUT_N)
            nc.vector.quantize_mx(
                out=v_codes[0, h].bitcast(FP8X4), scales=v_scales[:, 0, cols], in_=v_bf[0, h].rearrange("p e j -> p (e j)")
            )
        nc.vector.quantize_mx(
            out=rest_codes[:, 1:, :].rearrange("p h e -> p (h e)").bitcast(FP8X4),
            scales=v_scales[:, 1, :],
            in_=last_bf[:].rearrange("p e j -> p (e j)"),
        )

        inv_rows = psum.tile([P, Q], F32, name="score_bank0")
        nc.tensor.transpose(inv_rows[:], inv_sum[:].to_broadcast([P, P]), ident[:])
        factor = keep.tile([P, PASSES, PACK, Q], F32, tag="raw11", align_bytes=64)
        for g in range(PASSES):
            for j in range(PACK):
                nc.scalar.activation(out=factor[:, g, j, :], in_=inv_rows[:], func=ACT.Copy, scale=fac_cols[:, g, j : j + 1])
        dealt = keep.tile([P, PACK, P], F32, tag="dealt", align_bytes=64)
        nc.scalar.copy(
            out=dealt[:].rearrange("q j p -> q p j"), in_=placed_b[:, K_PASS:].rearrange("q (p j) -> q p j", j=PACK)
        )

        turned = [psum.tile([P, PACK, Q], F32, name=f"turned{g}") for g in range(PASSES)]
        for placed in (placed_lead, placed_a, placed_b):
            for g in range(PASSES):
                for j in range(PACK):
                    if placed is placed_b and g == 1:
                        columns = dealt[:, j, :]
                    else:
                        columns = placed[:, g * K_PASS + j : (g + 1) * K_PASS : PACK]
                    nc.tensor.matmul(
                        turned[g][:, j, :],
                        lhsT=columns,
                        rhs=ident[:],
                        start=(placed is placed_lead and j == 0),
                        stop=(placed is placed_b and j == PACK - 1),
                        is_transpose=True,
                    )

        w_bf = keep.tile([P, PASSES, Q, PACK], BF16, tag="mx_in1", align_bytes=64)
        w_codes = keep.tile([P, PASSES, Q], U32, tag="dealt", align_bytes=64)
        w_scales = keep.tile([P, PASSES, Q], U8, align_bytes=64)

        def weigh(g, rows):
            nc.vector.tensor_tensor(
                w_bf[:, g, rows, :],
                turned[g][:, :, rows].rearrange("p j q -> p q j"),
                factor[:, g, :, rows].rearrange("p j q -> p q j"),
                ALU.mult,
            )

        def quantize_weights(g):
            nc.vector.quantize_mx(
                out=w_codes[:, g, :].bitcast(FP8X4), scales=w_scales[:, g, :], in_=w_bf[:, g, :, :].rearrange("p q j -> p (q j)")
            )

        weigh(0, slice(0, Q))
        weigh(1, slice(0, Q // 2))
        quantize_weights(0)
        weigh(1, slice(Q // 2, Q))
        quantize_weights(1)

        out_banks = [psum.tile([P, OUT_N], F32, name=f"out_bank{h}") for h in range(E // OUT_N)]
        for g in range(PASSES):
            for h in range(E // OUT_N):
                cols = slice(h * OUT_N, (h + 1) * OUT_N)
                nc.tensor.matmul_mx(
                    out=out_banks[h][:],
                    lhsT=w_codes[:, g, :].bitcast(FP8X4),
                    lhsT_scale=w_scales[:, g, :],
                    rhs=v_codes[g, h].bitcast(FP8X4),
                    rhs_scale=v_scales[:, g, cols],
                    start=(g == 0),
                    stop=(g == PASSES - 1),
                )
        result = [keep.tile([P, OUT_N], F32, name=f"result{h}") for h in range(E // OUT_N)]
        nc.vector.tensor_copy(out=result[0][:], in_=out_banks[0][:])
        nc.sync.dma_start(out=out[:, 0:OUT_N], in_=result[0][:])
        nc.scalar.copy(out=result[1][:], in_=out_banks[1][:])
        nc.scalar.dma_start(out=out[:, OUT_N:E], in_=result[1][:])
